import numpy as np, ml_dtypes
CORES = [48,51,52,55]
N = 4
import mx_ref
BF = ml_dtypes.bfloat16
def entries(a):
    return np.ascontiguousarray(a.T).reshape(-1)
def table(e):
    return np.ascontiguousarray(np.reshape(e, (-1, 16)).T).astype(np.int32)
def cols(t, e):
    v = np.concatenate([t.reshape(128, -1, 4), np.zeros((128, 1, 4), BF)], axis=1)
    return np.ascontiguousarray(v[:, e]).reshape(128, -1)
def f(rng, *shape):
    return mx_ref.flush((rng.standard_normal(shape, dtype=np.float32) * np.exp2(rng.integers(-2, 3, shape[:-1] + (1,)))).astype(BF))
def wide(rng, *shape, cols=0):
    v = rng.standard_normal(shape, dtype=np.float32) * np.exp2(rng.integers(-12, 13, shape)).astype(np.float32)
    if cols: v *= np.repeat(np.exp2(rng.integers(-cols, cols + 1, shape[:-2] + (1, shape[-1] // 4))) * (rng.random(shape[:-2] + (1, shape[-1] // 4)) > 0.0625), 4, axis=-1).astype(np.float32)
    return mx_ref.flush(v.astype(BF))
T, S, CAPP, CL, K, O = 512, 512, 160, 160, 2048, 2
H = 65536 // (N * K)
def counts(rng, tot, cap, lead=None, least=2):
    n = np.full(N, least)
    if lead is not None:
        for i in range(N):
            q = (lead + i) % N; n[q] += min(cap - n[q], tot - n.sum())
    while n.sum() < tot:
        q = rng.integers(0, N)
        if n[q] < cap: n[q] += 1
    return n
def lists(rng, full=False, hot=False, other=False, few=False):
    a, b = rng.integers(1, N, 2); z = rng.integers(0, N); least = 0 if full else 2
    n = np.stack([counts(rng, T, CAPP, (r + a) % N if full or other else z if hot else None, least) for r in range(N)])
    part, pool = [], []
    for q in range(N):
        c = n[:, q].sum(); p = rng.permutation(K)[:c]
        key = q + N * (p + K * rng.integers(0, H, c))
        part.append(np.split(key, np.cumsum(n[:, q])[:-1])); pool.append(rng.choice(key, 1) if few else key)
    has = [np.concatenate([part[q][r] for q in range(N)]) for r in range(N)]
    ky, lk = [], []
    for r in range(N):
        ky.append(table(rng.permutation(has[r])))
        if other:
            s = (r + a) % N; e = rng.permutation(has[s])[:S]; m = np.bincount(e & (N - 1), minlength=N); e = [e]
            for q in ((s + a) % N, (s + a + 1) % N):
                more = rng.permutation(np.setdiff1d(pool[q], part[q][s]))[:CL - m[q]]
                e.append(more); m[q] += len(more)
            while m.sum() < S:
                q = rng.integers(0, N)
                if m[q] < CL: m[q] += 1; e.append(rng.choice(part[q][s], 1))
            u = np.unique(np.concatenate(e)); lead = part[(s + a) % N][s]
            assert len(lead) == CAPP and np.isin(lead, u).all()
            assert any(q != r and m[q] == CL and ((u & (N - 1)) == q).sum() == CL for q in range(N))
        else:
            m = counts(rng, S, CL, (r + b) % N if full else z if hot else None, least)
            e = [rng.choice(pool[q], m[q]) for q in range(N)]
        lk.append(table(rng.permutation(np.concatenate(e))))
    return {"ky": np.stack(ky), "lk": np.stack(lk)}
def setup_inputs(rng):
    d = lists(rng)
    return {"x": f(rng, N, 128, 4 * T), "ky": d["ky"], "lk": d["lk"], "w": f(rng, N, 128, 512 * O)}
def setup_inputs_full(rng):
    return {**setup_inputs(rng), **lists(rng, full=True)}
def setup_inputs_hot(rng):
    return {**setup_inputs(rng), **lists(rng, hot=True)}
def setup_inputs_other(rng):
    return {**setup_inputs(rng), **lists(rng, other=True)}
def setup_inputs_repeats(rng):
    return {**setup_inputs(rng), **lists(rng, few=True)}
def setup_inputs_spread(rng):
    d = setup_inputs(rng); d["x"] = wide(rng, N, 128, 4 * T, cols=8); return d
def check_inputs(d):
    b = []
    keys = np.stack([entries(d["ky"][r]) for r in range(N)]).astype(np.int64)
    if keys.min() < 0 or keys.max() > 65535: b.append("ky")
    if len(np.unique(keys & (N * K - 1))) != N * T: b.append("owner and place")
    for r in range(N):
        l = entries(d["lk"][r]).astype(np.int64)
        if np.bincount(keys[r] & (N - 1), minlength=N).max() > CAPP: b.append("CAPP")
        if not np.isin(l, keys).all(): b.append("lk")
        if np.bincount(l & (N - 1), minlength=N).max() > CL: b.append("CL")
    return b
def reference(x, ky, lk, w):
    every = np.concatenate([x[r] for r in range(N)], axis=1)
    number = np.full(65536, -1); number[np.concatenate([entries(ky[r]) for r in range(N)])] = np.arange(N * T)
    y = np.zeros((N, 128, O * S), np.float32)
    for r in range(N):
        v = mx_ref.quantize(cols(every, number[entries(lk[r])]))
        for o in range(O): y[r][:, S * o:S * o + S] = mx_ref.matmul(mx_ref.quantize(np.ascontiguousarray(w[r][:, 512 * o:512 * o + 512])), v)
    return {"y": y}

@@ -1,0 +1,244 @@
+from concourse.bass import DstId, RemoteDMATransfer
+from concourse.mybir import dt, AluOpType as A, ActivationFunctionType as F
+
+C8 = "float8_e4m3fn_x4"
+Z, TC, HC = 128, 512, 256
+DW = 8192
+WIN = Z + 2 * TC
+
+SCRATCH = {
+    "kr": ("sbuf", [128, 16], "int32"), "lr": ("sbuf", [128, 32], "int32"),
+    "ka": ("sbuf", [128, 16], "int32"), "la": ("sbuf", [128, 32], "int32"),
+    "ko": ("sbuf", [128, 16], "uint16"), "kp": ("sbuf", [128, 16], "uint16"),
+    "lo": ("sbuf", [128, 64], "uint16"), "rl": ("sbuf", [128, 64], "uint16"),
+    "pi": ("sbuf", [128, 1], "int32"), "b0": ("sbuf", [128, 1], "int32"), "g16": ("sbuf", [128, 1], "int32"),
+    "b0f": ("sbuf", [128, 1], "float32"), "af": ("sbuf", [128, 1], "float32"), "g256": ("sbuf", [128, 1], "float32"),
+    "lw": ("sbuf", [128, 128], "bfloat16"), "kb": ("sbuf", [128, 4], "float32"), "hb": ("sbuf", [128, 4], "float32"),
+    "vals": ("sbuf", [128, 512], "bfloat16"),
+    "tab": ("sbuf", [128, DW], "bfloat16"),
+    "zt": ("sbuf", [128, 512], "bfloat16"),
+    "xb": ("sbuf", [128, 4 * TC], "bfloat16"), "wt": ("sbuf", [128, 1024], "bfloat16"),
+    "wq": ("sbuf", [128, 256], C8), "ws": ("sbuf", [128, 256], "uint8"),
+    "pq": ("sbuf", [128, WIN], C8), "ps": ("sbuf", [128, WIN], "uint8"),
+    "sq": ("sbuf", [128, 2 * HC], C8), "ss": ("sbuf", [128, 2 * HC], "uint8"),
+    "oq": ("sbuf", [128, TC], C8), "os8": ("sbuf", [128, TC], "uint8"),
+    "aq": ("sbuf", [128, TC], C8), "as8": ("sbuf", [128, TC], "uint8"),
+    "ysb": ("sbuf", [128, 1024], "float32"),
+    "acc": ("psum", [128, 2048], "float32"),
+}
+for _n, _w in (("A", 1), ("B", 1), ("O", 2)):
+    SCRATCH["row" + _n] = ("sbuf", [128, 512 * _w], "bfloat16")
+    SCRATCH["tur" + _n] = ("sbuf", [128, 512 * _w], "bfloat16")
+    SCRATCH["sa" + _n] = ("sbuf", [128, 32 * _w], "float32")
+    SCRATCH["sb" + _n] = ("sbuf", [128, 16 * _w], "float32")
+    SCRATCH["of" + _n] = ("sbuf", [128, 16 * _w], "uint16")
+
+SEMAPHORES = ["kyl", "lkl", "xl0", "xl1", "wl", "cst", "zt", "dm0", "sdf", "v", "qz", "q0", "q1", "wqs", "ko", "lo",
+              "kpa", "rl0", "rl1", "tabs", "gA", "gB", "gO", "ofA", "ofB", "ofO", "p1", "pcA", "pcB", "pcO",
+              "psA", "psB", "psO", "ar0", "ar1", "mm00", "mm01", "mm10", "mm11",
+              "cp00", "cp01", "cp10", "cp11", "st0", "st1", "sent"]
+
+
+def rank_program(g, core, T, topo):
+    rank = T.rank_of(core)
+    if rank is None:
+        return
+    order = sorted(range(len(T.cores)), key=lambda r: (topo.die(T.cores[r]), r))
+    mine, others = (order[:2], order[2:]) if rank in order[:2] else (order[2:], order[:2])
+    k = mine.index(rank)
+    partner = T.cores[mine[1 - k]]
+    far = [T.cores[r] for r in others]
+    S = T.sem
+    V, SC, SY, TE = g.vector, g.scalar, g.sync, g.tensor
+    cnt = {"v": 0, "sent": 0}
+
+    def v(ins):
+        ins.then_inc(S.v, 1)
+        cnt["v"] += 1
+
+    def vw():
+        V.wait_ge(S.v, cnt["v"])
+
+    def engines(dst, part=0, parts=1):
+        e = topo.engines(core, dst)
+        n = len(e) // parts
+        return sum(1 << q for q in e[part * n:part * n + n]), n
+
+    def send(out, in_, sem, dst):
+        m, n = engines(dst)
+        rid, pid, _ = topo.addr(dst)
+        g.remote_dma(out, in_, S[sem], S.sent, pid, rid, m)
+        cnt["sent"] += n
+
+    nsend = len(topo.engines(core, partner))
+
+    own, par = Z, Z + TC
+    for q, u in ((SY, 0), (SC, 1)):
+        for j in range(4):
+            p = 16 * (2 * j + u)
+            q.dma_start(T.kr[p:p + 16, :], T.ky[:, 16 * u:16 * u + 16]).then_inc(S.kyl, 16)
+        for j in range(4):
+            p = 16 * (2 * j + u)
+            q.dma_start(T.lr[p:p + 16, :], T.lk[:]).then_inc(S.lkl, 16)
+        q.dma_start(T.xb[:, 1024 * u:1024 * u + 1024], T.x[:, 1024 * u:1024 * u + 1024]).then_inc(S["xl%d" % u], 16)
+    SY.dma_start(T.wt[:], T.w[:]).then_inc(S.wl, 16)
+
+    g.iota(T.pi[:], [[0, 1]], 0, 1).then_inc(S.cst, 1)
+    g.iota(T.kb[:], [[512, 2], [128, 2]], 128, 0, allow_small_or_imprecise_dtypes=True).then_inc(S.cst, 1)
+    g.iota(T.lw[:], [[1, 128]], 0, 0, allow_small_or_imprecise_dtypes=True).then_inc(S.cst, 1)
+    g.wait_ge(S.ko, 1)
+    send(T.kp[:], T.ko[:], "kpa", partner)
+    g.wait_ge(S.lo, 2)
+    tr = []
+    for i in range(2):
+        m, n = engines(far[i], i, 2)
+        rid, pid, _ = topo.addr(far[i])
+        tr.append(RemoteDMATransfer(dst_ids=[DstId(rid=rid, pnc=pid)], dma_engine_mask=m, remote_sem=S["rl%d" % k],
+                                    src=T.lo[:, 32 * i:32 * i + 32], dst=T.rl[:, 32 * k:32 * k + 32]))
+        cnt["sent"] += n
+    g.remote_dma_fused(tr, local_sem=S.sent)
+    for h in range(2):
+        g.wait_ge(S["q%d" % h], 1)
+        a, b = own + HC * h, par + HC * h
+        send(T.pq[:, b:b + HC].bitcast(dt.uint8), T.pq[:, a:a + HC].bitcast(dt.uint8), "p1", partner)
+        send(T.ps[:, b:b + HC], T.ps[:, a:a + HC], "p1", partner)
+    for n, a in (("A", k), ("B", 1 - k)):
+        c = HC * a
+        g.wait_ge(S["pc" + n], 1)
+        send(T.aq[:, HC * k:HC * k + HC].bitcast(dt.uint8), T.sq[:, c:c + HC].bitcast(dt.uint8), "ar%d" % k, far[a])
+        g.wait_ge(S["ps" + n], 1)
+        send(T.as8[:, HC * k:HC * k + HC], T.ss[:, c:c + HC], "ar%d" % k, far[a])
+    g.wait_ge(S.sent, cnt["sent"])
+
+    V.memset(T.zt[:], 0.0).then_inc(S.zt, 1)
+    V.memset(T.tab[:, 0:2048], 0.0).then_inc(S.dm0, 1)
+    V.wait_ge(S.cst, 3)
+    v(V.tensor_scalar(T.b0[:], T.pi[:], 1, None, A.bitwise_and))
+    v(V.tensor_scalar(T.g16[:], T.pi[:], 16, None, A.bitwise_and))
+    vw()
+    v(V.tensor_copy(T.b0f[:], T.b0[:]))
+    v(V.tensor_scalar(T.af[:], T.b0[:], -1.0, 1.0, A.mult, A.add))
+    v(V.tensor_scalar(T.g256[:], T.g16[:], 16.0, None, A.mult))
+    vw()
+    v(V.tensor_scalar(T.hb[:], T.kb[:], T.g256[:], T.b0f[:], A.add, A.mult))
+    vw()
+    for j in range(4):
+        v(V.tensor_scalar(T.vals[:, 128 * j:128 * j + 128], T.lw[:], T.af[:], T.hb[:, j:j + 1], A.mult, A.add))
+    V.wait_ge(S.zt, 1)
+    V.quantize_mx(T.pq[:, 0:Z], T.ps[:, 0:Z], T.zt[:]).then_inc(S.qz, 1)
+    v(V.memset(T.tab[:, 2048:3072], 0.0))
+    V.wait_ge(S.kyl, 128)
+    v(V.tensor_scalar(T.ka[:], T.kr[:], DW - 1, None, A.bitwise_and))
+    vw()
+    V.tensor_copy(T.ko[:], T.ka[:]).then_inc(S.ko, 1)
+    V.wait_ge(S.lkl, 128)
+    v(V.tensor_scalar(T.la[:], T.lr[:], DW - 1, None, A.bitwise_and))
+    vw()
+    V.tensor_copy(T.lo[:, 0:64:2], T.la[:]).then_inc(S.lo, 1)
+    V.tensor_copy(T.lo[:, 1:64:2], T.la[:]).then_inc(S.lo, 1)
+    v(V.memset(T.tab[:, 3072:6144], 0.0))
+    for h in range(2):
+        V.wait_ge(S["xl%d" % h], 16)
+        a = own + HC * h
+        V.quantize_mx(T.pq[:, a:a + HC], T.ps[:, a:a + HC], T.xb[:, 1024 * h:1024 * h + 1024]).then_inc(S["q%d" % h], 1)
+    V.wait_ge(S.dm0, 1)
+    V.wait_ge(S.sdf, 1)
+    V.wait_ge(S.ko, 1)
+    vw()
+    v(V.tensor_copy(T.tab[:, 0:DW].indirect(T.ko[:, 0:16]), T.vals[:, 0:256]))
+    V.wait_ge(S.wl, 16)
+    V.quantize_mx(T.wq[:], T.ws[:], T.wt[:]).then_inc(S.wqs, 1)
+    V.wait_ge(S.kpa, nsend)
+    vw()
+    V.tensor_copy(T.tab[:, 0:DW].indirect(T.kp[:, 0:16]), T.vals[:, 256:512]).then_inc(S.tabs, 1)
+    V.wait_ge(S.tabs, 1)
+
+    def turn(n, w, gs):
+        vw()
+        V.wait_ge(S["g" + n], gs)
+        row, tur, sa, sb, of = (T[b + n] for b in ("row", "tur", "sa", "sb", "of"))
+        v(V.transpose(tur[:], row[:]))
+        vw()
+        v(V.tensor_tensor(sa[:], tur[:, 0:512 * w:16], tur[:, 1:512 * w:16], A.add))
+        vw()
+        v(V.tensor_tensor(sb[:], sa[:, 0:32 * w:2], sa[:, 1:32 * w:2], A.add))
+        vw()
+        V.tensor_copy(of[:], sb[:]).then_inc(S["of" + n], 1)
+
+    nl = len(topo.engines(core, far[0])) // 2
+    rl = {"A": k, "B": 1 - k}
+    V.wait_ge(S["rl%d" % k], nl)
+    c = 32 * k
+    v(V.tensor_copy(T.rowA[:, 0:256], T.tab[:, 0:DW].indirect(T.rl[:, c:c + 16])))
+    turn("A", 1, 1)
+    turn("B", 1, 1)
+    V.wait_ge(S.qz, 1)
+    V.wait_ge(S.q0, 1)
+    V.wait_ge(S.q1, 1)
+    V.wait_ge(S.p1, 4 * nsend)
+    for n in ("A", "B"):
+        c = HC * rl[n]
+        V.wait_ge(S["of" + n], 1)
+        V.tensor_copy(T.sq[:, c:c + HC].bitcast(dt.uint32),
+                      T.pq[:, 0:WIN].bitcast(dt.uint32).indirect(T["of" + n][:, 0:16])).then_inc(S["pc" + n], 1)
+    V.wait_ge(S.lo, 2)
+    v(V.tensor_copy(T.rowO[:, 0:512], T.tab[:, 0:DW].indirect(T.lo[:, 0:32])))
+    turn("O", 2, 1)
+    V.wait_ge(S.ofO, 1)
+    V.tensor_copy(T.oq[:].bitcast(dt.uint32),
+                  T.pq[:, 0:WIN].bitcast(dt.uint32).indirect(T.ofO[:, 0:32])).then_inc(S.pcO, 1)
+    for c in (k, 1 - k):
+        V.wait_ge(S["mm0%d" % c], 1)
+        V.tensor_copy(T.ysb[:, HC * c:HC * c + HC],
+                      T.acc[:, 512 * c:512 * c + HC]).then_inc(S["cp0%d" % c], 1)
+
+    SC.wait_ge(S.dm0, 1)
+    SC.activation(T.tab[:, 6144:8192], T.tab[:, 0:2048], F.Copy).then_inc(S.sdf, 1)
+    SC.wait_ge(S.tabs, 1)
+    SC.wait_ge(S["rl%d" % k], nl)
+    c = 32 * k
+    SC.activation(T.rowA[:, 256:512], T.tab[:, 0:DW].indirect(T.rl[:, c + 16:c + 32]), F.Copy).then_inc(S.gA, 1)
+    SC.wait_ge(S["rl%d" % (1 - k)], nl)
+    c = 32 * (1 - k)
+    SC.activation(T.rowB[:], T.tab[:, 0:DW].indirect(T.rl[:, c:c + 32]), F.Copy).then_inc(S.gB, 1)
+    SC.wait_ge(S.qz, 1)
+    SC.wait_ge(S.q0, 1)
+    SC.wait_ge(S.q1, 1)
+    SC.wait_ge(S.p1, 4 * nsend)
+    for n in ("A", "B"):
+        c = HC * rl[n]
+        SC.wait_ge(S["of" + n], 1)
+        SC.activation(T.ss[:, c:c + HC], T.ps[:, 0:WIN].indirect(T["of" + n][:, 0:16]), F.Copy).then_inc(S["ps" + n], 1)
+    SC.wait_ge(S.lo, 2)
+    SC.activation(T.rowO[:, 512:1024], T.tab[:, 0:DW].indirect(T.lo[:, 32:64]), F.Copy).then_inc(S.gO, 1)
+    SC.wait_ge(S.ofO, 1)
+    SC.activation(T.os8[:], T.ps[:, 0:WIN].indirect(T.ofO[:, 0:32]), F.Copy).then_inc(S.psO, 1)
+    for c in (k, 1 - k):
+        SC.wait_ge(S["mm1%d" % c], 1)
+        a = 512 + HC * c
+        SC.activation(T.ysb[:, a:a + HC], T.acc[:, 1024 + 512 * c:1024 + 512 * c + HC], F.Copy).then_inc(S["cp1%d" % c], 1)
+        SC.wait_ge(S["cp1%d" % c], 1)
+        SC.dma_start(T.y[:, a:a + HC], T.ysb[:, a:a + HC]).then_inc(S.st1, 16)
+    SC.wait_ge(S.st1, 32)
+
+    TE.wait_ge(S.wqs, 1)
+    TE.wait_ge(S.pcO, 1)
+    TE.wait_ge(S.psO, 1)
+
+    def mm(o, c, q, s, first):
+        b = 1024 * o + 512 * c
+        return TE.matmul_mx(T.acc[:, b:b + HC], T.wq[:, 128 * o:128 * o + 128], T.ws[:, 128 * o:128 * o + 128],
+                            q[:, HC * c:HC * c + HC], s[:, HC * c:HC * c + HC], first, not first)
+
+    for c in (k, 1 - k):
+        for o in range(2):
+            mm(o, c, T.oq, T.os8, True)
+    for c in (k, 1 - k):
+        TE.wait_ge(S["ar%d" % c], 2 * nsend)
+        for o in range(2):
+            mm(o, c, T.aq, T.as8, False).then_inc(S["mm%d%d" % (o, c)], 1)
+
+    for c in (k, 1 - k):
+        SY.wait_ge(S["cp0%d" % c], 1)
+        SY.dma_start(T.y[:, HC * c:HC * c + HC], T.ysb[:, HC * c:HC * c + HC]).then_inc(S.st0, 16)
+    SY.wait_ge(S.st0, 32)

@@ -5,6 +5,12 @@ C8 = "float8_e4m3fn_x4"
 Z, TC, HC = 128, 512, 256
 DW = 8192
 WIN = Z + 2 * TC
+NX = 2
+XC = TC // NX
+FV = (0, 1024, 1664, 2944, 4096)
+FS = (4096, 5120, 6144, 7168, 7552)
+SEQV = ("tA", "pA", "tB", "pB", "tC", "pC", "tD", "pD")
+SEQS = ("gB", "pA", "gC", "pB", "gD", "pC", "pD")
 
 SCRATCH = {
     "kr": ("sbuf", [128, 16], "int32"), "lr": ("sbuf", [128, 32], "int32"),
@@ -26,17 +32,17 @@ SCRATCH = {
     "ysb": ("sbuf", [128, 1024], "float32"),
     "acc": ("psum", [128, 2048], "float32"),
 }
-for _n, _w in (("A", 1), ("B", 1), ("O", 2)):
-    SCRATCH["row" + _n] = ("sbuf", [128, 512 * _w], "bfloat16")
-    SCRATCH["tur" + _n] = ("sbuf", [128, 512 * _w], "bfloat16")
-    SCRATCH["sa" + _n] = ("sbuf", [128, 32 * _w], "float32")
-    SCRATCH["sb" + _n] = ("sbuf", [128, 16 * _w], "float32")
-    SCRATCH["of" + _n] = ("sbuf", [128, 16 * _w], "uint16")
+for _n in "ABCD":
+    SCRATCH["row" + _n] = ("sbuf", [128, 512], "bfloat16")
+    SCRATCH["tur" + _n] = ("sbuf", [128, 512], "bfloat16")
+    SCRATCH["sa" + _n] = ("sbuf", [128, 32], "float32")
+    SCRATCH["sb" + _n] = ("sbuf", [128, 16], "float32")
+    SCRATCH["of" + _n] = ("sbuf", [128, 16], "uint16")
 
-SEMAPHORES = ["kyl", "lkl", "xl0", "xl1", "wl", "cst", "zt", "dm0", "sdf", "v", "qz", "q0", "q1", "wqs", "ko", "lo",
-              "kpa", "rl0", "rl1", "tabs", "gA", "gB", "gO", "ofA", "ofB", "ofO", "p1", "pcA", "pcB", "pcO",
-              "psA", "psB", "psO", "ar0", "ar1", "mm00", "mm01", "mm10", "mm11",
-              "cp00", "cp01", "cp10", "cp11", "st0", "st1", "sent"]
+SEMAPHORES = ["kyl", "lkl", "wl", "cst", "gz", "zt", "dm0", "sdf", "v", "qz", "wqs", "ko", "lo", "kpa", "rl0", "rl1",
+              "tabs", "p1", "ar0", "ar1", "mm00", "mm01", "mm10", "mm11", "cp00", "cp01", "cp10", "cp11",
+              "st0", "st1", "sent"] + [s + str(h) for s in ("xl", "q") for h in range(NX)] + [
+              s + n for s in ("g", "of", "pc", "ps") for n in "ABCD"]
 
 
 def rank_program(g, core, T, topo):
@@ -71,6 +77,8 @@ def rank_program(g, core, T, topo):
         cnt["sent"] += n
 
     nsend = len(topo.engines(core, partner))
+    nl = nsend // 2
+    half = {"A": k, "B": 1 - k, "C": k, "D": 1 - k}
 
     own, par = Z, Z + TC
     for q, u in ((SY, 0), (SC, 1)):
@@ -80,12 +88,15 @@ def rank_program(g, core, T, topo):
         for j in range(4):
             p = 16 * (2 * j + u)
             q.dma_start(T.lr[p:p + 16, :], T.lk[:]).then_inc(S.lkl, 16)
-        q.dma_start(T.xb[:, 1024 * u:1024 * u + 1024], T.x[:, 1024 * u:1024 * u + 1024]).then_inc(S["xl%d" % u], 16)
+    for h in range(NX):
+        a = 4 * XC * h
+        SY.dma_start(T.xb[:, a:a + 4 * XC], T.x[:, a:a + 4 * XC]).then_inc(S["xl%d" % h], 16)
     SY.dma_start(T.wt[:], T.w[:]).then_inc(S.wl, 16)
 
     g.iota(T.pi[:], [[0, 1]], 0, 1).then_inc(S.cst, 1)
     g.iota(T.kb[:], [[512, 2], [128, 2]], 128, 0, allow_small_or_imprecise_dtypes=True).then_inc(S.cst, 1)
     g.iota(T.lw[:], [[1, 128]], 0, 0, allow_small_or_imprecise_dtypes=True).then_inc(S.cst, 1)
+    g.iota(T.tab[:, FS[-1]:DW], [[0, DW - FS[-1]]], 0, 0, allow_small_or_imprecise_dtypes=True).then_inc(S.gz, 1)
     g.wait_ge(S.ko, 1)
     send(T.kp[:], T.ko[:], "kpa", partner)
     g.wait_ge(S.lo, 2)
@@ -97,21 +108,35 @@ def rank_program(g, core, T, topo):
                                     src=T.lo[:, 32 * i:32 * i + 32], dst=T.rl[:, 32 * k:32 * k + 32]))
         cnt["sent"] += n
     g.remote_dma_fused(tr, local_sem=S.sent)
-    for h in range(2):
+    for h in range(NX):
         g.wait_ge(S["q%d" % h], 1)
-        a, b = own + HC * h, par + HC * h
-        send(T.pq[:, b:b + HC].bitcast(dt.uint8), T.pq[:, a:a + HC].bitcast(dt.uint8), "p1", partner)
-        send(T.ps[:, b:b + HC], T.ps[:, a:a + HC], "p1", partner)
-    for n, a in (("A", k), ("B", 1 - k)):
-        c = HC * a
+        a, b = own + XC * h, par + XC * h
+        send(T.pq[:, b:b + XC].bitcast(dt.uint8), T.pq[:, a:a + XC].bitcast(dt.uint8), "p1", partner)
+        send(T.ps[:, b:b + XC], T.ps[:, a:a + XC], "p1", partner)
+    for n in "AB":
+        c, dst = HC * half[n], far[half[n]]
         g.wait_ge(S["pc" + n], 1)
-        send(T.aq[:, HC * k:HC * k + HC].bitcast(dt.uint8), T.sq[:, c:c + HC].bitcast(dt.uint8), "ar%d" % k, far[a])
+        send(T.aq[:, HC * k:HC * k + HC].bitcast(dt.uint8), T.sq[:, c:c + HC].bitcast(dt.uint8), "ar%d" % k, dst)
         g.wait_ge(S["ps" + n], 1)
-        send(T.as8[:, HC * k:HC * k + HC], T.ss[:, c:c + HC], "ar%d" % k, far[a])
+        send(T.as8[:, HC * k:HC * k + HC], T.ss[:, c:c + HC], "ar%d" % k, dst)
     g.wait_ge(S.sent, cnt["sent"])
 
+    def window(q):
+        q.wait_ge(S.qz, 1)
+        for h in range(NX):
+            q.wait_ge(S["q%d" % h], 1)
+        q.wait_ge(S.p1, 2 * NX * nsend)
+
+    def asked(q, n):
+        q.wait_ge(S.tabs, 1)
+        if n in "AB":
+            q.wait_ge(S["rl%d" % half[n]], nl)
+        else:
+            q.wait_ge(S.lo, 2)
+        return (T.rl if n in "AB" else T.lo), 32 * half[n]
+
+    V.memset(T.tab[:, FV[0]:FV[1]], 0.0).then_inc(S.dm0, 1)
     V.memset(T.zt[:], 0.0).then_inc(S.zt, 1)
-    V.memset(T.tab[:, 0:2048], 0.0).then_inc(S.dm0, 1)
     V.wait_ge(S.cst, 3)
     v(V.tensor_scalar(T.b0[:], T.pi[:], 1, None, A.bitwise_and))
     v(V.tensor_scalar(T.g16[:], T.pi[:], 16, None, A.bitwise_and))
@@ -124,9 +149,7 @@ def rank_program(g, core, T, topo):
     vw()
     for j in range(4):
         v(V.tensor_scalar(T.vals[:, 128 * j:128 * j + 128], T.lw[:], T.af[:], T.hb[:, j:j + 1], A.mult, A.add))
-    V.wait_ge(S.zt, 1)
-    V.quantize_mx(T.pq[:, 0:Z], T.ps[:, 0:Z], T.zt[:]).then_inc(S.qz, 1)
-    v(V.memset(T.tab[:, 2048:3072], 0.0))
+    v(V.memset(T.tab[:, FV[1]:FV[2]], 0.0))
     V.wait_ge(S.kyl, 128)
     v(V.tensor_scalar(T.ka[:], T.kr[:], DW - 1, None, A.bitwise_and))
     vw()
@@ -136,83 +159,71 @@ def rank_program(g, core, T, topo):
     vw()
     V.tensor_copy(T.lo[:, 0:64:2], T.la[:]).then_inc(S.lo, 1)
     V.tensor_copy(T.lo[:, 1:64:2], T.la[:]).then_inc(S.lo, 1)
-    v(V.memset(T.tab[:, 3072:6144], 0.0))
-    for h in range(2):
+    for h in range(NX):
+        v(V.memset(T.tab[:, FV[2 + h]:FV[3 + h]], 0.0))
         V.wait_ge(S["xl%d" % h], 16)
-        a = own + HC * h
-        V.quantize_mx(T.pq[:, a:a + HC], T.ps[:, a:a + HC], T.xb[:, 1024 * h:1024 * h + 1024]).then_inc(S["q%d" % h], 1)
+        a = own + XC * h
+        V.quantize_mx(T.pq[:, a:a + XC], T.ps[:, a:a + XC],
+                      T.xb[:, 4 * XC * h:4 * XC * h + 4 * XC]).then_inc(S["q%d" % h], 1)
     V.wait_ge(S.dm0, 1)
-    V.wait_ge(S.sdf, 1)
+    V.wait_ge(S.gz, 1)
+    V.wait_ge(S.sdf, len(FS) - 1)
     V.wait_ge(S.ko, 1)
     vw()
     v(V.tensor_copy(T.tab[:, 0:DW].indirect(T.ko[:, 0:16]), T.vals[:, 0:256]))
+    V.wait_ge(S.zt, 1)
+    V.quantize_mx(T.pq[:, 0:Z], T.ps[:, 0:Z], T.zt[:]).then_inc(S.qz, 1)
     V.wait_ge(S.wl, 16)
     V.quantize_mx(T.wq[:], T.ws[:], T.wt[:]).then_inc(S.wqs, 1)
     V.wait_ge(S.kpa, nsend)
     vw()
     V.tensor_copy(T.tab[:, 0:DW].indirect(T.kp[:, 0:16]), T.vals[:, 256:512]).then_inc(S.tabs, 1)
-    V.wait_ge(S.tabs, 1)
-
-    def turn(n, w, gs):
-        vw()
-        V.wait_ge(S["g" + n], gs)
+    off, c = asked(V, "A")
+    v(V.tensor_copy(T.rowA[:, 0:256], T.tab[:, 0:DW].indirect(off[:, c:c + 16])))
+    first = [1]
+    for what, n in SEQV:
         row, tur, sa, sb, of = (T[b + n] for b in ("row", "tur", "sa", "sb", "of"))
-        v(V.transpose(tur[:], row[:]))
-        vw()
-        v(V.tensor_tensor(sa[:], tur[:, 0:512 * w:16], tur[:, 1:512 * w:16], A.add))
-        vw()
-        v(V.tensor_tensor(sb[:], sa[:, 0:32 * w:2], sa[:, 1:32 * w:2], A.add))
-        vw()
-        V.tensor_copy(of[:], sb[:]).then_inc(S["of" + n], 1)
-
-    nl = len(topo.engines(core, far[0])) // 2
-    rl = {"A": k, "B": 1 - k}
-    V.wait_ge(S["rl%d" % k], nl)
-    c = 32 * k
-    v(V.tensor_copy(T.rowA[:, 0:256], T.tab[:, 0:DW].indirect(T.rl[:, c:c + 16])))
-    turn("A", 1, 1)
-    turn("B", 1, 1)
-    V.wait_ge(S.qz, 1)
-    V.wait_ge(S.q0, 1)
-    V.wait_ge(S.q1, 1)
-    V.wait_ge(S.p1, 4 * nsend)
-    for n in ("A", "B"):
-        c = HC * rl[n]
-        V.wait_ge(S["of" + n], 1)
-        V.tensor_copy(T.sq[:, c:c + HC].bitcast(dt.uint32),
-                      T.pq[:, 0:WIN].bitcast(dt.uint32).indirect(T["of" + n][:, 0:16])).then_inc(S["pc" + n], 1)
-    V.wait_ge(S.lo, 2)
-    v(V.tensor_copy(T.rowO[:, 0:512], T.tab[:, 0:DW].indirect(T.lo[:, 0:32])))
-    turn("O", 2, 1)
-    V.wait_ge(S.ofO, 1)
-    V.tensor_copy(T.oq[:].bitcast(dt.uint32),
-                  T.pq[:, 0:WIN].bitcast(dt.uint32).indirect(T.ofO[:, 0:32])).then_inc(S.pcO, 1)
+        if what == "t":
+            vw()
+            V.wait_ge(S["g" + n], 1)
+            v(V.transpose(tur[:], row[:]))
+            vw()
+            v(V.tensor_tensor(sa[:], tur[:, 0:512:16], tur[:, 1:512:16], A.add))
+            vw()
+            v(V.tensor_tensor(sb[:], sa[:, 0:32:2], sa[:, 1:32:2], A.add))
+            vw()
+            V.tensor_copy(of[:], sb[:]).then_inc(S["of" + n], 1)
+        else:
+            if first[0]:
+                window(V)
+                first[0] = 0
+            V.wait_ge(S["of" + n], 1)
+            c, out = HC * half[n], (T.sq if n in "AB" else T.oq)
+            V.tensor_copy(out[:, c:c + HC].bitcast(dt.uint32),
+                          T.pq[:, 0:WIN].bitcast(dt.uint32).indirect(of[:, 0:16])).then_inc(S["pc" + n], 1)
     for c in (k, 1 - k):
         V.wait_ge(S["mm0%d" % c], 1)
         V.tensor_copy(T.ysb[:, HC * c:HC * c + HC],
                       T.acc[:, 512 * c:512 * c + HC]).then_inc(S["cp0%d" % c], 1)
 
     SC.wait_ge(S.dm0, 1)
-    SC.activation(T.tab[:, 6144:8192], T.tab[:, 0:2048], F.Copy).then_inc(S.sdf, 1)
-    SC.wait_ge(S.tabs, 1)
-    SC.wait_ge(S["rl%d" % k], nl)
-    c = 32 * k
-    SC.activation(T.rowA[:, 256:512], T.tab[:, 0:DW].indirect(T.rl[:, c + 16:c + 32]), F.Copy).then_inc(S.gA, 1)
-    SC.wait_ge(S["rl%d" % (1 - k)], nl)
-    c = 32 * (1 - k)
-    SC.activation(T.rowB[:], T.tab[:, 0:DW].indirect(T.rl[:, c:c + 32]), F.Copy).then_inc(S.gB, 1)
-    SC.wait_ge(S.qz, 1)
-    SC.wait_ge(S.q0, 1)
-    SC.wait_ge(S.q1, 1)
-    SC.wait_ge(S.p1, 4 * nsend)
-    for n in ("A", "B"):
-        c = HC * rl[n]
-        SC.wait_ge(S["of" + n], 1)
-        SC.activation(T.ss[:, c:c + HC], T.ps[:, 0:WIN].indirect(T["of" + n][:, 0:16]), F.Copy).then_inc(S["ps" + n], 1)
-    SC.wait_ge(S.lo, 2)
-    SC.activation(T.rowO[:, 512:1024], T.tab[:, 0:DW].indirect(T.lo[:, 32:64]), F.Copy).then_inc(S.gO, 1)
-    SC.wait_ge(S.ofO, 1)
-    SC.activation(T.os8[:], T.ps[:, 0:WIN].indirect(T.ofO[:, 0:32]), F.Copy).then_inc(S.psO, 1)
+    for a, b in zip(FS, FS[1:]):
+        SC.activation(T.tab[:, a:b], T.tab[:, 0:b - a], F.Copy).then_inc(S.sdf, 1)
+    off, c = asked(SC, "A")
+    SC.activation(T.rowA[:, 256:512], T.tab[:, 0:DW].indirect(off[:, c + 16:c + 32]), F.Copy).then_inc(S.gA, 1)
+    first = [1]
+    for what, n in SEQS:
+        if what == "g":
+            off, c = asked(SC, n)
+            SC.activation(T["row" + n][:], T.tab[:, 0:DW].indirect(off[:, c:c + 32]), F.Copy).then_inc(S["g" + n], 1)
+        else:
+            if first[0]:
+                window(SC)
+                first[0] = 0
+            SC.wait_ge(S["of" + n], 1)
+            c, out = HC * half[n], (T.ss if n in "AB" else T.os8)
+            SC.activation(out[:, c:c + HC], T.ps[:, 0:WIN].indirect(T["of" + n][:, 0:16]),
+                          F.Copy).then_inc(S["ps" + n], 1)
     for c in (k, 1 - k):
         SC.wait_ge(S["mm1%d" % c], 1)
         a = 512 + HC * c
@@ -221,19 +232,18 @@ def rank_program(g, core, T, topo):
         SC.dma_start(T.y[:, a:a + HC], T.ysb[:, a:a + HC]).then_inc(S.st1, 16)
     SC.wait_ge(S.st1, 32)
 
-    TE.wait_ge(S.wqs, 1)
-    TE.wait_ge(S.pcO, 1)
-    TE.wait_ge(S.psO, 1)
-
     def mm(o, c, q, s, first):
         b = 1024 * o + 512 * c
         return TE.matmul_mx(T.acc[:, b:b + HC], T.wq[:, 128 * o:128 * o + 128], T.ws[:, 128 * o:128 * o + 128],
                             q[:, HC * c:HC * c + HC], s[:, HC * c:HC * c + HC], first, not first)
 
-    for c in (k, 1 - k):
+    TE.wait_ge(S.wqs, 1)
+    for n in "CD":
+        c = half[n]
+        TE.wait_ge(S["pc" + n], 1)
+        TE.wait_ge(S["ps" + n], 1)
         for o in range(2):
             mm(o, c, T.oq, T.os8, True)
-    for c in (k, 1 - k):
         TE.wait_ge(S["ar%d" % c], 2 * nsend)
         for o in range(2):
             mm(o, c, T.aq, T.as8, False).then_inc(S["mm%d%d" % (o, c)], 1)

@@ -7,10 +7,12 @@ DW = 8192
 WIN = Z + 2 * TC
 NX = 2
 XC = TC // NX
-FV = (0, 1024, 1664, 2944, 4096)
-FS = (4096, 5120, 6144, 7168, 7552)
-SEQV = ("tA", "pA", "tB", "pB", "tC", "pC", "tD", "pD")
-SEQS = ("gB", "pA", "gC", "pB", "gD", "pC", "pD")
+FV = (0, 1024, 1408, 2624, 3840)
+FS = (3840, 4864, 5888, 6912, 7552)
+PART = {"0": (0, 16), "1": (16, 32), "f": (0, 32)}
+SEQV = ("gA0", "gB0", "tA", "tB", "1A", "1B", "2A", "2B", "cA", "cB", "pA", "tC", "pB", "1C", "2C", "cC", "w-", "tD",
+        "pC", "1D", "2D", "cD", "pD")
+SEQS = ("gA1", "gB1", "gCf", "gDf", "pA", "pB", "pC", "pD")
 
 SCRATCH = {
     "kr": ("sbuf", [128, 16], "int32"), "lr": ("sbuf", [128, 32], "int32"),
@@ -39,10 +41,10 @@ for _n in "ABCD":
     SCRATCH["sb" + _n] = ("sbuf", [128, 16], "float32")
     SCRATCH["of" + _n] = ("sbuf", [128, 16], "uint16")
 
-SEMAPHORES = ["kyl", "lkl", "wl", "cst", "gz", "zt", "dm0", "sdf", "v", "qz", "wqs", "ko", "lo", "kpa", "rl0", "rl1",
+SEMAPHORES = ["kyl", "lkl", "wl", "cst", "gz", "zt", "dm0", "sdf", "v", "qz", "wqs", "ko", "lo", "kar", "rl0", "rl1",
               "tabs", "p1", "ar0", "ar1", "mm00", "mm01", "mm10", "mm11", "cp00", "cp01", "cp10", "cp11",
               "st0", "st1", "sent"] + [s + str(h) for s in ("xl", "q") for h in range(NX)] + [
-              s + n for s in ("g", "of", "pc", "ps") for n in "ABCD"]
+              s + n for s in ("g", "v", "of", "pc", "ps") for n in "ABCD"]
 
 
 def rank_program(g, core, T, topo):
@@ -98,7 +100,7 @@ def rank_program(g, core, T, topo):
     g.iota(T.lw[:], [[1, 128]], 0, 0, allow_small_or_imprecise_dtypes=True).then_inc(S.cst, 1)
     g.iota(T.tab[:, FS[-1]:DW], [[0, DW - FS[-1]]], 0, 0, allow_small_or_imprecise_dtypes=True).then_inc(S.gz, 1)
     g.wait_ge(S.ko, 1)
-    send(T.kp[:], T.ko[:], "kpa", partner)
+    send(T.kp[:], T.ko[:], "kar", partner)
     g.wait_ge(S.lo, 2)
     tr = []
     for i in range(2):
@@ -173,27 +175,23 @@ def rank_program(g, core, T, topo):
     v(V.tensor_copy(T.tab[:, 0:DW].indirect(T.ko[:, 0:16]), T.vals[:, 0:256]))
     V.wait_ge(S.zt, 1)
     V.quantize_mx(T.pq[:, 0:Z], T.ps[:, 0:Z], T.zt[:]).then_inc(S.qz, 1)
-    V.wait_ge(S.wl, 16)
-    V.quantize_mx(T.wq[:], T.ws[:], T.wt[:]).then_inc(S.wqs, 1)
-    V.wait_ge(S.kpa, nsend)
+    V.wait_ge(S.kar, nsend)
     vw()
     V.tensor_copy(T.tab[:, 0:DW].indirect(T.kp[:, 0:16]), T.vals[:, 256:512]).then_inc(S.tabs, 1)
-    off, c = asked(V, "A")
-    v(V.tensor_copy(T.rowA[:, 0:256], T.tab[:, 0:DW].indirect(off[:, c:c + 16])))
     first = [1]
-    for what, n in SEQV:
+    done = {n: 0 for n in "ABCD"}
+    for op in SEQV:
+        what, n = op[0], op[1]
+        if what == "w":
+            V.wait_ge(S.wl, 16)
+            V.quantize_mx(T.wq[:], T.ws[:], T.wt[:]).then_inc(S.wqs, 1)
+            continue
         row, tur, sa, sb, of = (T[b + n] for b in ("row", "tur", "sa", "sb", "of"))
-        if what == "t":
-            vw()
-            V.wait_ge(S["g" + n], 1)
-            v(V.transpose(tur[:], row[:]))
-            vw()
-            v(V.tensor_tensor(sa[:], tur[:, 0:512:16], tur[:, 1:512:16], A.add))
-            vw()
-            v(V.tensor_tensor(sb[:], sa[:, 0:32:2], sa[:, 1:32:2], A.add))
-            vw()
-            V.tensor_copy(of[:], sb[:]).then_inc(S["of" + n], 1)
-        else:
+        if what == "g":
+            off, c = asked(V, n)
+            a, b = PART[op[2]]
+            ins = V.tensor_copy(row[:, 16 * a:16 * b], T.tab[:, 0:DW].indirect(off[:, c + a:c + b]))
+        elif what == "p":
             if first[0]:
                 window(V)
                 first[0] = 0
@@ -201,6 +199,22 @@ def rank_program(g, core, T, topo):
             c, out = HC * half[n], (T.sq if n in "AB" else T.oq)
             V.tensor_copy(out[:, c:c + HC].bitcast(dt.uint32),
                           T.pq[:, 0:WIN].bitcast(dt.uint32).indirect(of[:, 0:16])).then_inc(S["pc" + n], 1)
+            continue
+        else:
+            if done[n]:
+                V.wait_ge(S["v" + n], done[n])
+            if what == "t":
+                V.wait_ge(S["g" + n], 1)
+                ins = V.transpose(tur[:], row[:])
+            elif what == "1":
+                ins = V.tensor_tensor(sa[:], tur[:, 0:512:16], tur[:, 1:512:16], A.add)
+            elif what == "2":
+                ins = V.tensor_tensor(sb[:], sa[:, 0:32:2], sa[:, 1:32:2], A.add)
+            else:
+                V.tensor_copy(of[:], sb[:]).then_inc(S["of" + n], 1)
+                continue
+        ins.then_inc(S["v" + n], 1)
+        done[n] += 1
     for c in (k, 1 - k):
         V.wait_ge(S["mm0%d" % c], 1)
         V.tensor_copy(T.ysb[:, HC * c:HC * c + HC],
@@ -209,13 +223,14 @@ def rank_program(g, core, T, topo):
     SC.wait_ge(S.dm0, 1)
     for a, b in zip(FS, FS[1:]):
         SC.activation(T.tab[:, a:b], T.tab[:, 0:b - a], F.Copy).then_inc(S.sdf, 1)
-    off, c = asked(SC, "A")
-    SC.activation(T.rowA[:, 256:512], T.tab[:, 0:DW].indirect(off[:, c + 16:c + 32]), F.Copy).then_inc(S.gA, 1)
     first = [1]
-    for what, n in SEQS:
+    for op in SEQS:
+        what, n = op[0], op[1]
         if what == "g":
             off, c = asked(SC, n)
-            SC.activation(T["row" + n][:], T.tab[:, 0:DW].indirect(off[:, c:c + 32]), F.Copy).then_inc(S["g" + n], 1)
+            a, b = PART[op[2]]
+            SC.activation(T["row" + n][:, 16 * a:16 * b], T.tab[:, 0:DW].indirect(off[:, c + a:c + b]),
+                          F.Copy).then_inc(S["g" + n], 1)
         else:
             if first[0]:
                 window(SC)

@@ -2,16 +2,17 @@ from concourse.bass import DstId, RemoteDMATransfer
 from concourse.mybir import dt, AluOpType as A, ActivationFunctionType as F
 
 C8 = "float8_e4m3fn_x4"
-Z, TC, HC = 128, 512, 256
+Z, TC, HC = 16, 512, 256
 DW = 8192
 WIN = Z + 2 * TC
 NX = 2
 XC = TC // NX
-FV = (0, 1024, 1408, 2624, 3840)
-FS = (3840, 4864, 5888, 6912, 7552)
+FV = (0, 768, 2048, 2816, 3840, 4992)
+FS = (4992, 5632, 6400, 7168, 7680)
+PRE = ("h", "z3", "z1", "k", "v0", "K", "l", "v1", "L", "z2", "z4", "q0", "s0", "q1", "s1")
 PART = {"0": (0, 16), "1": (16, 32), "f": (0, 32)}
-SEQV = ("gA0", "gB0", "tA", "tB", "1A", "1B", "2A", "2B", "cA", "cB", "pA", "tC", "pB", "1C", "2C", "cC", "w-", "tD",
-        "pC", "1D", "2D", "cD", "pD")
+SEQV = ("gA0", "gB0", "tA", "tB", "sA", "sB", "cA", "cB", "pA", "tC", "pB", "sC", "tD", "cC", "sD", "w-", "cD",
+        "pC", "pD")
 SEQS = ("gA1", "gB1", "gCf", "gDf", "pA", "pB", "pC", "pD")
 
 SCRATCH = {
@@ -19,13 +20,11 @@ SCRATCH = {
     "ka": ("sbuf", [128, 16], "int32"), "la": ("sbuf", [128, 32], "int32"),
     "ko": ("sbuf", [128, 16], "uint16"), "kp": ("sbuf", [128, 16], "uint16"),
     "lo": ("sbuf", [128, 64], "uint16"), "rl": ("sbuf", [128, 64], "uint16"),
-    "pi": ("sbuf", [128, 1], "int32"), "b0": ("sbuf", [128, 1], "int32"), "g16": ("sbuf", [128, 1], "int32"),
-    "b0f": ("sbuf", [128, 1], "float32"), "af": ("sbuf", [128, 1], "float32"), "g256": ("sbuf", [128, 1], "float32"),
-    "lw": ("sbuf", [128, 128], "bfloat16"), "kb": ("sbuf", [128, 4], "float32"), "hb": ("sbuf", [128, 4], "float32"),
+    "hr": ("sbuf", [128, 64], "float32"), "hc": ("sbuf", [128, 64], "float32"), "cap": ("sbuf", [128, 64], "float32"),
+    "lw": ("sbuf", [128, 256], "bfloat16"),
     "vals": ("sbuf", [128, 512], "bfloat16"),
     "tab": ("sbuf", [128, DW], "bfloat16"),
-    "zt": ("sbuf", [128, 512], "bfloat16"),
-    "xb": ("sbuf", [128, 4 * TC], "bfloat16"), "wt": ("sbuf", [128, 1024], "bfloat16"),
+    "xb": ("sbuf", [128, 4 * (Z + TC)], "bfloat16"), "wt": ("sbuf", [128, 1024], "bfloat16"),
     "wq": ("sbuf", [128, 256], C8), "ws": ("sbuf", [128, 256], "uint8"),
     "pq": ("sbuf", [128, WIN], C8), "ps": ("sbuf", [128, WIN], "uint8"),
     "sq": ("sbuf", [128, 2 * HC], C8), "ss": ("sbuf", [128, 2 * HC], "uint8"),
@@ -37,13 +36,13 @@ SCRATCH = {
 for _n in "ABCD":
     SCRATCH["row" + _n] = ("sbuf", [128, 512], "bfloat16")
     SCRATCH["tur" + _n] = ("sbuf", [128, 512], "bfloat16")
-    SCRATCH["sa" + _n] = ("sbuf", [128, 32], "float32")
-    SCRATCH["sb" + _n] = ("sbuf", [128, 16], "float32")
+    SCRATCH["su" + _n] = ("sbuf", [128, 64], "float32")
     SCRATCH["of" + _n] = ("sbuf", [128, 16], "uint16")
 
-SEMAPHORES = ["kyl", "lkl", "wl", "cst", "gz", "zt", "dm0", "sdf", "v", "qz", "wqs", "ko", "lo", "kar", "rl0", "rl1",
-              "tabs", "p1", "ar0", "ar1", "mm00", "mm01", "mm10", "mm11", "cp00", "cp01", "cp10", "cp11",
-              "st0", "st1", "sent"] + [s + str(h) for s in ("xl", "q") for h in range(NX)] + [
+SEMAPHORES = ["kyl", "lkl", "wl", "hr", "hc", "lw", "cap", "va", "gz", "xz", "dm0", "vz", "sdf", "ka", "la", "sc", "wqs",
+              "ko", "lo", "kar", "rl0", "rl1", "tabs", "p1", "ar0", "ar1", "mm00", "mm01", "mm10", "mm11",
+              "cp00", "cp01", "cp10", "cp11", "st0", "st1", "sent"] + [
+              s + str(h) for s in ("xl", "q") for h in range(NX)] + [
               s + n for s in ("g", "v", "of", "pc", "ps") for n in "ABCD"]
 
 
@@ -58,14 +57,7 @@ def rank_program(g, core, T, topo):
     far = [T.cores[r] for r in others]
     S = T.sem
     V, SC, SY, TE = g.vector, g.scalar, g.sync, g.tensor
-    cnt = {"v": 0, "sent": 0}
-
-    def v(ins):
-        ins.then_inc(S.v, 1)
-        cnt["v"] += 1
-
-    def vw():
-        V.wait_ge(S.v, cnt["v"])
+    cnt = {"sent": 0}
 
     def engines(dst, part=0, parts=1):
         e = topo.engines(core, dst)
@@ -92,13 +84,17 @@ def rank_program(g, core, T, topo):
             q.dma_start(T.lr[p:p + 16, :], T.lk[:]).then_inc(S.lkl, 16)
     for h in range(NX):
         a = 4 * XC * h
-        SY.dma_start(T.xb[:, a:a + 4 * XC], T.x[:, a:a + 4 * XC]).then_inc(S["xl%d" % h], 16)
+        SY.dma_start(T.xb[:, 4 * Z + a:4 * Z + a + 4 * XC], T.x[:, a:a + 4 * XC]).then_inc(S["xl%d" % h], 16)
+    SY.wait_ge(S.tabs, 1)
     SY.dma_start(T.wt[:], T.w[:]).then_inc(S.wl, 16)
 
-    g.iota(T.pi[:], [[0, 1]], 0, 1).then_inc(S.cst, 1)
-    g.iota(T.kb[:], [[512, 2], [128, 2]], 128, 0, allow_small_or_imprecise_dtypes=True).then_inc(S.cst, 1)
-    g.iota(T.lw[:], [[1, 128]], 0, 0, allow_small_or_imprecise_dtypes=True).then_inc(S.cst, 1)
-    g.iota(T.tab[:, FS[-1]:DW], [[0, DW - FS[-1]]], 0, 0, allow_small_or_imprecise_dtypes=True).then_inc(S.gz, 1)
+    def iota(out, pattern, base, sem):
+        g.iota(out, pattern, base, 0, allow_small_or_imprecise_dtypes=True).then_inc(S[sem], 1)
+
+    iota(T.hr[:], [[TC, 2], [HC, 2], [256, 16]], Z + 256 - 8 * 256, "hr")
+    iota(T.lw[:], [[1, HC]], -256, "lw")
+    iota(T.cap[:], [[0, 16], [2048, 4]], 0, "cap")
+    iota(T.tab[:, FS[-1]:DW], [[0, DW - FS[-1]]], 0, "gz")
     g.wait_ge(S.ko, 1)
     send(T.kp[:], T.ko[:], "kar", partner)
     g.wait_ge(S.lo, 2)
@@ -124,7 +120,6 @@ def rank_program(g, core, T, topo):
     g.wait_ge(S.sent, cnt["sent"])
 
     def window(q):
-        q.wait_ge(S.qz, 1)
         for h in range(NX):
             q.wait_ge(S["q%d" % h], 1)
         q.wait_ge(S.p1, 2 * NX * nsend)
@@ -138,46 +133,51 @@ def rank_program(g, core, T, topo):
         return (T.rl if n in "AB" else T.lo), 32 * half[n]
 
     V.memset(T.tab[:, FV[0]:FV[1]], 0.0).then_inc(S.dm0, 1)
-    V.memset(T.zt[:], 0.0).then_inc(S.zt, 1)
-    V.wait_ge(S.cst, 3)
-    v(V.tensor_scalar(T.b0[:], T.pi[:], 1, None, A.bitwise_and))
-    v(V.tensor_scalar(T.g16[:], T.pi[:], 16, None, A.bitwise_and))
-    vw()
-    v(V.tensor_copy(T.b0f[:], T.b0[:]))
-    v(V.tensor_scalar(T.af[:], T.b0[:], -1.0, 1.0, A.mult, A.add))
-    v(V.tensor_scalar(T.g256[:], T.g16[:], 16.0, None, A.mult))
-    vw()
-    v(V.tensor_scalar(T.hb[:], T.kb[:], T.g256[:], T.b0f[:], A.add, A.mult))
-    vw()
-    for j in range(4):
-        v(V.tensor_scalar(T.vals[:, 128 * j:128 * j + 128], T.lw[:], T.af[:], T.hb[:, j:j + 1], A.mult, A.add))
-    v(V.memset(T.tab[:, FV[1]:FV[2]], 0.0))
-    V.wait_ge(S.kyl, 128)
-    v(V.tensor_scalar(T.ka[:], T.kr[:], DW - 1, None, A.bitwise_and))
-    vw()
-    V.tensor_copy(T.ko[:], T.ka[:]).then_inc(S.ko, 1)
-    V.wait_ge(S.lkl, 128)
-    v(V.tensor_scalar(T.la[:], T.lr[:], DW - 1, None, A.bitwise_and))
-    vw()
-    V.tensor_copy(T.lo[:, 0:64:2], T.la[:]).then_inc(S.lo, 1)
-    V.tensor_copy(T.lo[:, 1:64:2], T.la[:]).then_inc(S.lo, 1)
-    for h in range(NX):
-        v(V.memset(T.tab[:, FV[2 + h]:FV[3 + h]], 0.0))
-        V.wait_ge(S["xl%d" % h], 16)
-        a = own + XC * h
-        V.quantize_mx(T.pq[:, a:a + XC], T.ps[:, a:a + XC],
-                      T.xb[:, 4 * XC * h:4 * XC * h + 4 * XC]).then_inc(S["q%d" % h], 1)
-    V.wait_ge(S.dm0, 1)
-    V.wait_ge(S.gz, 1)
-    V.wait_ge(S.sdf, len(FS) - 1)
-    V.wait_ge(S.ko, 1)
-    vw()
-    v(V.tensor_copy(T.tab[:, 0:DW].indirect(T.ko[:, 0:16]), T.vals[:, 0:256]))
-    V.wait_ge(S.zt, 1)
-    V.quantize_mx(T.pq[:, 0:Z], T.ps[:, 0:Z], T.zt[:]).then_inc(S.qz, 1)
-    V.wait_ge(S.kar, nsend)
-    vw()
-    V.tensor_copy(T.tab[:, 0:DW].indirect(T.kp[:, 0:16]), T.vals[:, 256:512]).then_inc(S.tabs, 1)
+    V.memset(T.xb[:, 0:4 * Z], 0.0).then_inc(S.xz, 1)
+    for op in PRE:
+        what, i = op[0], int(op[1:] or 0)
+        if what == "z":
+            V.memset(T.tab[:, FV[i]:FV[i + 1]], 0.0).then_inc(S.vz, 1)
+        elif what == "h":
+            V.wait_ge(S.hr, 1)
+            V.transpose(T.hc[:], T.hr[:]).then_inc(S.hc, 1)
+        elif what == "v":
+            V.wait_ge(S.lw, 1)
+            V.wait_ge(S.hc, 1)
+            V.tensor_scalar(T.vals[:, HC * i:HC * i + HC], T.lw[:], T.hc[:, 32 * i:32 * i + 1], None,
+                            A.max).then_inc(S.va, 1)
+        elif what == "k":
+            V.wait_ge(S.kyl, 128)
+            V.tensor_scalar(T.ka[:], T.kr[:], DW - 1, None, A.bitwise_and).then_inc(S.ka, 1)
+        elif what == "K":
+            V.wait_ge(S.ka, 1)
+            V.tensor_copy(T.ko[:], T.ka[:]).then_inc(S.ko, 1)
+        elif what == "l":
+            V.wait_ge(S.lkl, 128)
+            V.tensor_scalar(T.la[:], T.lr[:], DW - 1, None, A.bitwise_and).then_inc(S.la, 1)
+        elif what == "L":
+            V.wait_ge(S.la, 1)
+            for d in range(2):
+                V.tensor_copy(T.lo[:, d:64:2], T.la[:]).then_inc(S.lo, 1)
+        elif what == "q":
+            V.wait_ge(S["xl%d" % i], 16)
+            if i == 0:
+                V.wait_ge(S.xz, 1)
+            a, b = (own + XC * i if i else 0), own + XC * i + XC
+            V.quantize_mx(T.pq[:, a:b], T.ps[:, a:b], T.xb[:, 4 * a:4 * b]).then_inc(S["q%d" % i], 1)
+        elif i == 0:
+            V.wait_ge(S.dm0, 1)
+            V.wait_ge(S.vz, len(FV) - 2)
+            V.wait_ge(S.gz, 1)
+            V.wait_ge(S.sdf, len(FS) - 1)
+            V.wait_ge(S.ko, 1)
+            V.wait_ge(S.va, 2)
+            V.tensor_copy(T.tab[:, 0:DW].indirect(T.ko[:, 0:16]), T.vals[:, 0:HC]).then_inc(S.sc, 1)
+        else:
+            V.wait_ge(S.kar, nsend)
+            V.wait_ge(S.sc, 1)
+            V.tensor_copy(T.tab[:, 0:DW].indirect(T.kp[:, 0:16]), T.vals[:, HC:2 * HC]).then_inc(S.tabs, 1)
+
     first = [1]
     done = {n: 0 for n in "ABCD"}
     for op in SEQV:
@@ -186,7 +186,7 @@ def rank_program(g, core, T, topo):
             V.wait_ge(S.wl, 16)
             V.quantize_mx(T.wq[:], T.ws[:], T.wt[:]).then_inc(S.wqs, 1)
             continue
-        row, tur, sa, sb, of = (T[b + n] for b in ("row", "tur", "sa", "sb", "of"))
+        row, tur, su, of = (T[b + n] for b in ("row", "tur", "su", "of"))
         if what == "g":
             off, c = asked(V, n)
             a, b = PART[op[2]]
@@ -204,14 +204,14 @@ def rank_program(g, core, T, topo):
             if done[n]:
                 V.wait_ge(S["v" + n], done[n])
             if what == "t":
-                V.wait_ge(S["g" + n], 1)
+                if any(s[:2] == "g" + n for s in SEQS):
+                    V.wait_ge(S["g" + n], 1)
                 ins = V.transpose(tur[:], row[:])
-            elif what == "1":
-                ins = V.tensor_tensor(sa[:], tur[:, 0:512:16], tur[:, 1:512:16], A.add)
-            elif what == "2":
-                ins = V.tensor_tensor(sb[:], sa[:, 0:32:2], sa[:, 1:32:2], A.add)
+            elif what == "s":
+                V.wait_ge(S.cap, 1)
+                ins = V.tensor_tensor_scan(su[:], T.cap[:], tur[:, 0:512:8], 0.0, A.min, A.add)
             else:
-                V.tensor_copy(of[:], sb[:]).then_inc(S["of" + n], 1)
+                V.tensor_copy(of[:], su[:, 3:64:4]).then_inc(S["of" + n], 1)
                 continue
         ins.then_inc(S["v" + n], 1)
         done[n] += 1
@@ -259,6 +259,8 @@ def rank_program(g, core, T, topo):
         TE.wait_ge(S["ps" + n], 1)
         for o in range(2):
             mm(o, c, T.oq, T.os8, True)
+    for n in "CD":
+        c = half[n]
         TE.wait_ge(S["ar%d" % c], 2 * nsend)
         for o in range(2):
             mm(o, c, T.aq, T.as8, False).then_inc(S["mm%d%d" % (o, c)], 1)

@@ -7,13 +7,14 @@ DW = 8192
 WIN = Z + 2 * TC
 NX = 2
 XC = TC // NX
-FV = (0, 768, 2048, 2816, 3840, 4992)
-FS = (4992, 5632, 6400, 7168, 7680)
+FV = (0, 768, 2048, 2816, 3584, 4736)
+FS = (4736, 5504, 6272, 7040, 7680)
 PRE = ("h", "z3", "z1", "k", "v0", "K", "l", "v1", "L", "z2", "z4", "q0", "s0", "q1", "s1")
 PART = {"0": (0, 16), "1": (16, 32), "f": (0, 32)}
 SEQV = ("gA0", "gB0", "tA", "tB", "sA", "sB", "cA", "cB", "pA", "tC", "pB", "sC", "tD", "cC", "sD", "w-", "cD",
         "pC", "pD")
 SEQS = ("gA1", "gB1", "gCf", "gDf", "pA", "pB", "pC", "pD")
+SEQT = ("Ca", "Co", "Do", "Da")
 
 SCRATCH = {
     "kr": ("sbuf", [128, 16], "int32"), "lr": ("sbuf", [128, 32], "int32"),
@@ -76,9 +77,9 @@ def rank_program(g, core, T, topo):
 
     own, par = Z, Z + TC
     for q, u in ((SY, 0), (SC, 1)):
-        for j in range(4):
-            p = 16 * (2 * j + u)
-            q.dma_start(T.kr[p:p + 16, :], T.ky[:, 16 * u:16 * u + 16]).then_inc(S.kyl, 16)
+        for j in range(2):
+            p = 32 * (2 * j + u)
+            q.dma_start(T.kr[p:p + 32, :], T.ky[:]).then_inc(S.kyl, 16)
         for j in range(4):
             p = 16 * (2 * j + u)
             q.dma_start(T.lr[p:p + 16, :], T.lk[:]).then_inc(S.lkl, 16)
@@ -91,8 +92,8 @@ def rank_program(g, core, T, topo):
     def iota(out, pattern, base, sem):
         g.iota(out, pattern, base, 0, allow_small_or_imprecise_dtypes=True).then_inc(S[sem], 1)
 
-    iota(T.hr[:], [[TC, 2], [HC, 2], [256, 16]], Z + 256 - 8 * 256, "hr")
-    iota(T.lw[:], [[1, HC]], -256, "lw")
+    iota(T.hr[:], [[TC, 2], [8, 2], [256, 16]], Z + 256 - 8 * 256, "hr")
+    iota(T.lw[:], [[16, 16], [1, 8], [256, 2]], -256, "lw")
     iota(T.cap[:], [[0, 16], [2048, 4]], 0, "cap")
     iota(T.tab[:, FS[-1]:DW], [[0, DW - FS[-1]]], 0, "gz")
     g.wait_ge(S.ko, 1)
@@ -147,7 +148,7 @@ def rank_program(g, core, T, topo):
             V.tensor_scalar(T.vals[:, HC * i:HC * i + HC], T.lw[:], T.hc[:, 32 * i:32 * i + 1], None,
                             A.max).then_inc(S.va, 1)
         elif what == "k":
-            V.wait_ge(S.kyl, 128)
+            V.wait_ge(S.kyl, 64)
             V.tensor_scalar(T.ka[:], T.kr[:], DW - 1, None, A.bitwise_and).then_inc(S.ka, 1)
         elif what == "K":
             V.wait_ge(S.ka, 1)
@@ -247,23 +248,25 @@ def rank_program(g, core, T, topo):
         SC.dma_start(T.y[:, a:a + HC], T.ysb[:, a:a + HC]).then_inc(S.st1, 16)
     SC.wait_ge(S.st1, 32)
 
-    def mm(o, c, q, s, first):
-        b = 1024 * o + 512 * c
-        return TE.matmul_mx(T.acc[:, b:b + HC], T.wq[:, 128 * o:128 * o + 128], T.ws[:, 128 * o:128 * o + 128],
-                            q[:, HC * c:HC * c + HC], s[:, HC * c:HC * c + HC], first, not first)
-
     TE.wait_ge(S.wqs, 1)
-    for n in "CD":
-        c = half[n]
-        TE.wait_ge(S["pc" + n], 1)
-        TE.wait_ge(S["ps" + n], 1)
+    begun = []
+    for op in SEQT:
+        n, c = op[0], half[op[0]]
+        begin = n not in begun
+        begun.append(n)
+        if op[1] == "o":
+            q, s = T.oq, T.os8
+            TE.wait_ge(S["pc" + n], 1)
+            TE.wait_ge(S["ps" + n], 1)
+        else:
+            q, s = T.aq, T.as8
+            TE.wait_ge(S["ar%d" % c], 2 * nsend)
         for o in range(2):
-            mm(o, c, T.oq, T.os8, True)
-    for n in "CD":
-        c = half[n]
-        TE.wait_ge(S["ar%d" % c], 2 * nsend)
-        for o in range(2):
-            mm(o, c, T.aq, T.as8, False).then_inc(S["mm%d%d" % (o, c)], 1)
+            b = 1024 * o + 512 * c
+            ins = TE.matmul_mx(T.acc[:, b:b + HC], T.wq[:, 128 * o:128 * o + 128], T.ws[:, 128 * o:128 * o + 128],
+                               q[:, HC * c:HC * c + HC], s[:, HC * c:HC * c + HC], begin, not begin)
+            if not begin:
+                ins.then_inc(S["mm%d%d" % (o, c)], 1)
 
     for c in (k, 1 - k):
         SY.wait_ge(S["cp0%d" % c], 1)

from concourse.bass import DstId, RemoteDMATransfer
from concourse.mybir import dt, AluOpType as A, ActivationFunctionType as F

C8 = "float8_e4m3fn_x4"
Z, TC, HC = 16, 512, 256
DW = 8192
WIN = Z + 2 * TC
NX = 2
XC = TC // NX
FV = (0, 768, 2048, 2816, 3584, 4736)
FS = (4736, 5504, 6272, 7040, 7680)
PRE = ("h", "z3", "z1", "k", "v0", "K", "l", "v1", "L", "z2", "z4", "q0", "s0", "q1", "s1")
PART = {"0": (0, 16), "1": (16, 32), "f": (0, 32)}
SEQV = ("gA0", "gB0", "tA", "tB", "sA", "sB", "cA", "cB", "pA", "tC", "pB", "sC", "tD", "cC", "sD", "w-", "cD",
        "pC", "pD")
SEQS = ("gA1", "gB1", "gCf", "gDf", "pA", "pB", "pC", "pD")
SEQT = ("Ca", "Co", "Do", "Da")

SCRATCH = {
    "kr": ("sbuf", [128, 16], "int32"), "lr": ("sbuf", [128, 32], "int32"),
    "ka": ("sbuf", [128, 16], "int32"), "la": ("sbuf", [128, 32], "int32"),
    "ko": ("sbuf", [128, 16], "uint16"), "kp": ("sbuf", [128, 16], "uint16"),
    "lo": ("sbuf", [128, 64], "uint16"), "rl": ("sbuf", [128, 64], "uint16"),
    "hr": ("sbuf", [128, 64], "float32"), "hc": ("sbuf", [128, 64], "float32"), "cap": ("sbuf", [128, 64], "float32"),
    "lw": ("sbuf", [128, 256], "bfloat16"),
    "vals": ("sbuf", [128, 512], "bfloat16"),
    "tab": ("sbuf", [128, DW], "bfloat16"),
    "xb": ("sbuf", [128, 4 * (Z + TC)], "bfloat16"), "wt": ("sbuf", [128, 1024], "bfloat16"),
    "wq": ("sbuf", [128, 256], C8), "ws": ("sbuf", [128, 256], "uint8"),
    "pq": ("sbuf", [128, WIN], C8), "ps": ("sbuf", [128, WIN], "uint8"),
    "sq": ("sbuf", [128, 2 * HC], C8), "ss": ("sbuf", [128, 2 * HC], "uint8"),
    "oq": ("sbuf", [128, TC], C8), "os8": ("sbuf", [128, TC], "uint8"),
    "aq": ("sbuf", [128, TC], C8), "as8": ("sbuf", [128, TC], "uint8"),
    "ysb": ("sbuf", [128, 1024], "float32"),
    "acc": ("psum", [128, 2048], "float32"),
}
for _n in "ABCD":
    SCRATCH["row" + _n] = ("sbuf", [128, 512], "bfloat16")
    SCRATCH["tur" + _n] = ("sbuf", [128, 512], "bfloat16")
    SCRATCH["su" + _n] = ("sbuf", [128, 64], "float32")
    SCRATCH["of" + _n] = ("sbuf", [128, 16], "uint16")

SEMAPHORES = ["kyl", "lkl", "wl", "hr", "hc", "lw", "cap", "va", "gz", "xz", "dm0", "vz", "sdf", "ka", "la", "sc", "wqs",
              "ko", "lo", "kar", "rl0", "rl1", "tabs", "p1", "ar0", "ar1", "mm00", "mm01", "mm10", "mm11",
              "cp00", "cp01", "cp10", "cp11", "st0", "st1", "sent"] + [
              s + str(h) for s in ("xl", "q") for h in range(NX)] + [
              s + n for s in ("g", "v", "of", "pc", "ps") for n in "ABCD"]


def rank_program(g, core, T, topo):
    rank = T.rank_of(core)
    if rank is None:
        return
    order = sorted(range(len(T.cores)), key=lambda r: (topo.die(T.cores[r]), r))
    mine, others = (order[:2], order[2:]) if rank in order[:2] else (order[2:], order[:2])
    k = mine.index(rank)
    partner = T.cores[mine[1 - k]]
    far = [T.cores[r] for r in others]
    S = T.sem
    V, SC, SY, TE = g.vector, g.scalar, g.sync, g.tensor
    cnt = {"sent": 0}

    def engines(dst, part=0, parts=1):
        e = topo.engines(core, dst)
        n = len(e) // parts
        return sum(1 << q for q in e[part * n:part * n + n]), n

    def send(out, in_, sem, dst):
        m, n = engines(dst)
        rid, pid, _ = topo.addr(dst)
        g.remote_dma(out, in_, S[sem], S.sent, pid, rid, m)
        cnt["sent"] += n

    nsend = len(topo.engines(core, partner))
    nl = nsend // 2
    half = {"A": k, "B": 1 - k, "C": k, "D": 1 - k}

    own, par = Z, Z + TC
    for q, u in ((SY, 0), (SC, 1)):
        for j in range(2):
            p = 32 * (2 * j + u)
            q.dma_start(T.kr[p:p + 32, :], T.ky[:]).then_inc(S.kyl, 16)
        for j in range(4):
            p = 16 * (2 * j + u)
            q.dma_start(T.lr[p:p + 16, :], T.lk[:]).then_inc(S.lkl, 16)
    for h in range(NX):
        a = 4 * XC * h
        SY.dma_start(T.xb[:, 4 * Z + a:4 * Z + a + 4 * XC], T.x[:, a:a + 4 * XC]).then_inc(S["xl%d" % h], 16)
    SY.wait_ge(S.tabs, 1)
    SY.dma_start(T.wt[:], T.w[:]).then_inc(S.wl, 16)

    def iota(out, pattern, base, sem):
        g.iota(out, pattern, base, 0, allow_small_or_imprecise_dtypes=True).then_inc(S[sem], 1)

    iota(T.hr[:], [[TC, 2], [8, 2], [256, 16]], Z + 256 - 8 * 256, "hr")
    iota(T.lw[:], [[16, 16], [1, 8], [256, 2]], -256, "lw")
    iota(T.cap[:], [[0, 16], [2048, 4]], 0, "cap")
    iota(T.tab[:, FS[-1]:DW], [[0, DW - FS[-1]]], 0, "gz")
    g.wait_ge(S.ko, 1)
    send(T.kp[:], T.ko[:], "kar", partner)
    g.wait_ge(S.lo, 2)
    tr = []
    for i in range(2):
        m, n = engines(far[i], i, 2)
        rid, pid, _ = topo.addr(far[i])
        tr.append(RemoteDMATransfer(dst_ids=[DstId(rid=rid, pnc=pid)], dma_engine_mask=m, remote_sem=S["rl%d" % k],
                                    src=T.lo[:, 32 * i:32 * i + 32], dst=T.rl[:, 32 * k:32 * k + 32]))
        cnt["sent"] += n
    g.remote_dma_fused(tr, local_sem=S.sent)
    for h in range(NX):
        g.wait_ge(S["q%d" % h], 1)
        a, b = own + XC * h, par + XC * h
        send(T.pq[:, b:b + XC].bitcast(dt.uint8), T.pq[:, a:a + XC].bitcast(dt.uint8), "p1", partner)
        send(T.ps[:, b:b + XC], T.ps[:, a:a + XC], "p1", partner)
    for n in "AB":
        c, dst = HC * half[n], far[half[n]]
        g.wait_ge(S["pc" + n], 1)
        send(T.aq[:, HC * k:HC * k + HC].bitcast(dt.uint8), T.sq[:, c:c + HC].bitcast(dt.uint8), "ar%d" % k, dst)
        g.wait_ge(S["ps" + n], 1)
        send(T.as8[:, HC * k:HC * k + HC], T.ss[:, c:c + HC], "ar%d" % k, dst)
    g.wait_ge(S.sent, cnt["sent"])

    def window(q):
        for h in range(NX):
            q.wait_ge(S["q%d" % h], 1)
        q.wait_ge(S.p1, 2 * NX * nsend)

    def asked(q, n):
        q.wait_ge(S.tabs, 1)
        if n in "AB":
            q.wait_ge(S["rl%d" % half[n]], nl)
        else:
            q.wait_ge(S.lo, 2)
        return (T.rl if n in "AB" else T.lo), 32 * half[n]

    V.memset(T.tab[:, FV[0]:FV[1]], 0.0).then_inc(S.dm0, 1)
    V.memset(T.xb[:, 0:4 * Z], 0.0).then_inc(S.xz, 1)
    for op in PRE:
        what, i = op[0], int(op[1:] or 0)
        if what == "z":
            V.memset(T.tab[:, FV[i]:FV[i + 1]], 0.0).then_inc(S.vz, 1)
        elif what == "h":
            V.wait_ge(S.hr, 1)
            V.transpose(T.hc[:], T.hr[:]).then_inc(S.hc, 1)
        elif what == "v":
            V.wait_ge(S.lw, 1)
            V.wait_ge(S.hc, 1)
            V.tensor_scalar(T.vals[:, HC * i:HC * i + HC], T.lw[:], T.hc[:, 32 * i:32 * i + 1], None,
                            A.max).then_inc(S.va, 1)
        elif what == "k":
            V.wait_ge(S.kyl, 64)
            V.tensor_scalar(T.ka[:], T.kr[:], DW - 1, None, A.bitwise_and).then_inc(S.ka, 1)
        elif what == "K":
            V.wait_ge(S.ka, 1)
            V.tensor_copy(T.ko[:], T.ka[:]).then_inc(S.ko, 1)
        elif what == "l":
            V.wait_ge(S.lkl, 128)
            V.tensor_scalar(T.la[:], T.lr[:], DW - 1, None, A.bitwise_and).then_inc(S.la, 1)
        elif what == "L":
            V.wait_ge(S.la, 1)
            for d in range(2):
                V.tensor_copy(T.lo[:, d:64:2], T.la[:]).then_inc(S.lo, 1)
        elif what == "q":
            V.wait_ge(S["xl%d" % i], 16)
            if i == 0:
                V.wait_ge(S.xz, 1)
            a, b = (own + XC * i if i else 0), own + XC * i + XC
            V.quantize_mx(T.pq[:, a:b], T.ps[:, a:b], T.xb[:, 4 * a:4 * b]).then_inc(S["q%d" % i], 1)
        elif i == 0:
            V.wait_ge(S.dm0, 1)
            V.wait_ge(S.vz, len(FV) - 2)
            V.wait_ge(S.gz, 1)
            V.wait_ge(S.sdf, len(FS) - 1)
            V.wait_ge(S.ko, 1)
            V.wait_ge(S.va, 2)
            V.tensor_copy(T.tab[:, 0:DW].indirect(T.ko[:, 0:16]), T.vals[:, 0:HC]).then_inc(S.sc, 1)
        else:
            V.wait_ge(S.kar, nsend)
            V.wait_ge(S.sc, 1)
            V.tensor_copy(T.tab[:, 0:DW].indirect(T.kp[:, 0:16]), T.vals[:, HC:2 * HC]).then_inc(S.tabs, 1)

    first = [1]
    done = {n: 0 for n in "ABCD"}
    for op in SEQV:
        what, n = op[0], op[1]
        if what == "w":
            V.wait_ge(S.wl, 16)
            V.quantize_mx(T.wq[:], T.ws[:], T.wt[:]).then_inc(S.wqs, 1)
            continue
        row, tur, su, of = (T[b + n] for b in ("row", "tur", "su", "of"))
        if what == "g":
            off, c = asked(V, n)
            a, b = PART[op[2]]
            ins = V.tensor_copy(row[:, 16 * a:16 * b], T.tab[:, 0:DW].indirect(off[:, c + a:c + b]))
        elif what == "p":
            if first[0]:
                window(V)
                first[0] = 0
            V.wait_ge(S["of" + n], 1)
            c, out = HC * half[n], (T.sq if n in "AB" else T.oq)
            V.tensor_copy(out[:, c:c + HC].bitcast(dt.uint32),
                          T.pq[:, 0:WIN].bitcast(dt.uint32).indirect(of[:, 0:16])).then_inc(S["pc" + n], 1)
            continue
        else:
            if done[n]:
                V.wait_ge(S["v" + n], done[n])
            if what == "t":
                if any(s[:2] == "g" + n for s in SEQS):
                    V.wait_ge(S["g" + n], 1)
                ins = V.transpose(tur[:], row[:])
            elif what == "s":
                V.wait_ge(S.cap, 1)
                ins = V.tensor_tensor_scan(su[:], T.cap[:], tur[:, 0:512:8], 0.0, A.min, A.add)
            else:
                V.tensor_copy(of[:], su[:, 3:64:4]).then_inc(S["of" + n], 1)
                continue
        ins.then_inc(S["v" + n], 1)
        done[n] += 1
    for c in (k, 1 - k):
        V.wait_ge(S["mm0%d" % c], 1)
        V.tensor_copy(T.ysb[:, HC * c:HC * c + HC],
                      T.acc[:, 512 * c:512 * c + HC]).then_inc(S["cp0%d" % c], 1)

    SC.wait_ge(S.dm0, 1)
    for a, b in zip(FS, FS[1:]):
        SC.activation(T.tab[:, a:b], T.tab[:, 0:b - a], F.Copy).then_inc(S.sdf, 1)
    first = [1]
    for op in SEQS:
        what, n = op[0], op[1]
        if what == "g":
            off, c = asked(SC, n)
            a, b = PART[op[2]]
            SC.activation(T["row" + n][:, 16 * a:16 * b], T.tab[:, 0:DW].indirect(off[:, c + a:c + b]),
                          F.Copy).then_inc(S["g" + n], 1)
        else:
            if first[0]:
                window(SC)
                first[0] = 0
            SC.wait_ge(S["of" + n], 1)
            c, out = HC * half[n], (T.ss if n in "AB" else T.os8)
            SC.activation(out[:, c:c + HC], T.ps[:, 0:WIN].indirect(T["of" + n][:, 0:16]),
                          F.Copy).then_inc(S["ps" + n], 1)
    for c in (k, 1 - k):
        SC.wait_ge(S["mm1%d" % c], 1)
        a = 512 + HC * c
        SC.activation(T.ysb[:, a:a + HC], T.acc[:, 1024 + 512 * c:1024 + 512 * c + HC], F.Copy).then_inc(S["cp1%d" % c], 1)
        SC.wait_ge(S["cp1%d" % c], 1)
        SC.dma_start(T.y[:, a:a + HC], T.ysb[:, a:a + HC]).then_inc(S.st1, 16)
    SC.wait_ge(S.st1, 32)

    TE.wait_ge(S.wqs, 1)
    begun = []
    for op in SEQT:
        n, c = op[0], half[op[0]]
        begin = n not in begun
        begun.append(n)
        if op[1] == "o":
            q, s = T.oq, T.os8
            TE.wait_ge(S["pc" + n], 1)
            TE.wait_ge(S["ps" + n], 1)
        else:
            q, s = T.aq, T.as8
            TE.wait_ge(S["ar%d" % c], 2 * nsend)
        for o in range(2):
            b = 1024 * o + 512 * c
            ins = TE.matmul_mx(T.acc[:, b:b + HC], T.wq[:, 128 * o:128 * o + 128], T.ws[:, 128 * o:128 * o + 128],
                               q[:, HC * c:HC * c + HC], s[:, HC * c:HC * c + HC], begin, not begin)
            if not begin:
                ins.then_inc(S["mm%d%d" % (o, c)], 1)

    for c in (k, 1 - k):
        SY.wait_ge(S["cp0%d" % c], 1)
        SY.dma_start(T.y[:, HC * c:HC * c + HC], T.ysb[:, HC * c:HC * c + HC]).then_inc(S.st0, 16)
    SY.wait_ge(S.st0, 32)
